import numpy as np
import ml_dtypes


def mxq(x, axis, fmt="e4m3"):
    dtype, down = {"e4m3": (ml_dtypes.float8_e4m3fn, 7), "e5m2": (ml_dtypes.float8_e5m2, 14)}[fmt]
    v = np.moveaxis(np.asarray(x, np.float32).astype(ml_dtypes.bfloat16).astype(np.float64), axis, -1)
    blocks = v.reshape(v.shape[:-1] + (-1, 32))
    amax = np.abs(blocks).max(-1, keepdims=True)
    byte = np.maximum(np.where(amax > 0, np.frexp(amax)[1] - 1 + 127, 0) - down, 1)
    scale = np.exp2(byte - 127.0)
    codes = (blocks / scale).astype(np.float32).astype(dtype).astype(np.float64)
    return np.moveaxis((codes * scale).reshape(v.shape), -1, axis)


WIDE = False


def mx_kscale(k):
    if not WIDE:
        return np.ones(k)
    levels = np.array([10, -10, 5, -5, 0])
    if k % 512:
        return np.exp2(np.random.permutation(np.resize(levels, k // 32))).repeat(32)
    a = np.empty((k // 512, 16))
    for p in range(k // 512):
        a[p, :8] = np.random.permutation(np.resize(levels, 8))
        for g in range(8):
            far = levels[np.abs(levels - a[p, g]) >= 10]
            a[p, g + 8] = far[np.random.randint(len(far))]
    return np.exp2(a.ravel()).repeat(32)


BF16 = ml_dtypes.bfloat16


def bf(x):
    return np.asarray(x, np.float32).astype(BF16)


def f64(x):
    return np.asarray(x).astype(np.float64)


N, D, C, O = 8192, 512, 512, 256


def centre_logits(x, a, m, p, lp):
    h = x * a
    k = (x * x - 1.0) * a
    hm = mxq(h, 1, "e4m3") @ mxq(m, 0, "e4m3")
    kp = mxq(k, 1, "e4m3") @ mxq(p, 0, "e4m3")
    return hm - kp + lp


def draw0():
    s, t = mx_kscale(D), mx_kscale(C)
    return {
        "x": bf(np.random.standard_normal((N, D))),
        "a": bf((1.0 + 0.1 * np.random.standard_normal(D)) * s),
        "m": bf(np.random.standard_normal((D, C)) * (0.7 / np.sqrt(D)) / s[:, None]),
        "p": bf(np.random.standard_normal((D, C)) * (0.5 / np.sqrt(D)) / s[:, None]),
        "lp": bf(0.3 * np.random.standard_normal(C)),
        "gc": bf((1.0 + 0.1 * np.random.standard_normal(C)) * t),
        "w": bf(np.random.standard_normal((C, O)) / np.sqrt(C) / t[:, None]),
    }


def core(x, a, m, p, lp, gc, w):
    q = centre_logits(f64(x), f64(a), f64(m), f64(p), f64(lp))
    e = np.exp(q - q.max(-1, keepdims=True))
    phi = e / e.sum(-1, keepdims=True)
    num_centres = phi.shape[-1]
    r = (num_centres * phi - 1.0) * f64(gc)
    return mxq(r, 1, "e4m3") @ mxq(f64(w), 0, "e4m3")


def e4m3fn_bytes(y):
    return np.clip(np.asarray(y, np.float64), -448.0, 448.0).astype(np.float32).astype(ml_dtypes.float8_e4m3fn).view(np.uint8)


def e4m3fn_values(b):
    return np.asarray(b, np.uint8).view(ml_dtypes.float8_e4m3fn).astype(np.float64)


def setup_inputs():
    d = draw0()
    x0 = np.asarray(d['p']).astype(np.float64)
    s = (np.max(np.abs(x0), axis=(1,), keepdims=True) / 448.0).astype(np.float32)
    out = {}
    for k, v in d.items():
        if k == 'p':
            out['p_bytes'] = e4m3fn_bytes(x0 / s.astype(np.float64))
            out['p_scale'] = s
        else:
            out[k] = v
    return out


def reference(x, a, m, p_bytes, p_scale, lp, gc, w):
    return core(x, a, m, e4m3fn_values(p_bytes) * p_scale.astype(np.float64), lp, gc, w)

@@ -1,0 +1,265 @@
+from contextlib import ExitStack
+
+import concourse.mybir as mybir
+from concourse.masks import make_identity
+
+N, D, C, O = 8192, 512, 512, 256
+FLOPS = 2 * N * D * C * 2 + 2 * N * C * O
+
+F32 = mybir.dt.float32
+BF16 = mybir.dt.bfloat16
+U32 = mybir.dt.uint32
+U8 = mybir.dt.uint8
+FP8 = mybir.dt.float8_e4m3fn
+FP8X4 = mybir.dt.float8_e4m3fn_x4
+ACT = mybir.ActivationFunctionType
+ALU = mybir.AluOpType
+AX = mybir.AxisListType
+
+P = 128
+PACK = 4
+J = 2
+TOK = J * P
+PAIRS = N // TOK
+
+ORDER = [
+    ("TX", 0), ("SQ", 0), ("TQ0", 2), ("R0", 3), ("TQ1", 2), ("TU1", 3), ("QZ", 1), ("M0", 2), ("E0", 2), ("M1", 2),
+    ("R1", 3), ("QA", 1), ("E1", 2), ("C0", 2), ("QR", 3), ("H", 0), ("LA", 1), ("C1", 2), ("QB", 1), ("K", 0),
+    ("LB", 1), ("U0", 2), ("OU", 3), ("U1", 2), ("TU0", 2), ("CO", 3),
+]
+
+
+def tile_ellipticalnormalizedrbfnet_t_kernel(tc, x, a, m, p_bytes, p_scale, lp, gc, w, out):
+    nc = tc.nc
+    x_v = x.rearrange("(g p j) d -> g p j d", p=P, j=J)
+    out_v = out.rearrange("(g p j) o -> g p j o", p=P, j=J)
+
+    with ExitStack() as ctx:
+        keep = ctx.enter_context(tc.tile_pool(name="keep", bufs=1))
+        xin = ctx.enter_context(tc.tile_pool(name="xin", bufs=6))
+        work = ctx.enter_context(tc.tile_pool(name="work", bufs=3))
+        psum = ctx.enter_context(tc.psum_pool(name="psum", bufs=2))
+
+        x_tiles = {}
+
+        def load(i):
+            x_sb = xin.tile([P, J, D], BF16, name="x_sb")
+            nc.sync.dma_start(out=x_sb[:], in_=x_v[i])
+            x_tiles[i] = x_sb
+
+        ident = keep.tile([P, P], F32, name="ident")
+        make_identity(nc, ident[:])
+        warm = keep.tile([P, 1], F32, name="warm")
+        nc.gpsimd.memset(warm[:], 0.0)
+        warm2 = keep.tile([P, 1], F32, name="warm2")
+        nc.scalar.activation(out=warm2[:], in_=warm[:], func=ACT.Exp, bias=0.0, scale=1.0)
+
+        load(0)
+        a_sb = keep.tile([P, PACK], BF16, name="a_sb")
+        nc.sync.dma_start(out=a_sb[:], in_=a.rearrange("(p t) -> p t", t=PACK))
+        ps_sb = keep.tile([P, PACK], F32, name="ps_sb")
+        nc.sync.dma_start(out=ps_sb[:], in_=p_scale.rearrange("(p t) o -> p (t o)", t=PACK))
+        pb_sb = keep.tile([P, PACK, C], U8, name="pb_sb")
+        nc.sync.dma_start(out=pb_sb[:], in_=p_bytes.rearrange("(p t) c -> p t c", t=PACK))
+        m_sb = keep.tile([P, PACK, C], BF16, name="m_sb")
+        nc.sync.dma_start(out=m_sb[:], in_=m.rearrange("(p t) c -> p t c", t=PACK))
+        lp_sb = keep.tile([P, PACK], BF16, name="lp_sb")
+        nc.sync.dma_start(out=lp_sb[:], in_=lp.rearrange("(p t) -> p t", t=PACK))
+        gc_sb = keep.tile([P, PACK], BF16, name="gc_sb")
+        nc.sync.dma_start(out=gc_sb[:], in_=gc.rearrange("(p t) -> p t", t=PACK))
+        load(1)
+        w_sb = keep.tile([P, PACK, O], BF16, name="w_sb")
+        nc.sync.dma_start(out=w_sb[:], in_=w.rearrange("(p t) o -> p t o", t=PACK))
+        load(2)
+        load(3)
+
+        a_rep = keep.tile([P, TOK, PACK], BF16, name="a_rep", align_bytes=64)
+        nc.gpsimd.tensor_scalar(
+            out=a_rep[:], in0=a_sb[:].unsqueeze(1).to_broadcast([P, TOK, PACK]), scalar1=1.0, scalar2=0.0, op0=ALU.mult, op1=ALU.add
+        )
+        gc_rep = keep.tile([P, P, PACK], F32, name="gc_rep", align_bytes=64)
+        nc.gpsimd.tensor_scalar(
+            out=gc_rep[:], in0=gc_sb[:].unsqueeze(1).to_broadcast([P, P, PACK]), scalar1=float(C), scalar2=0.0, op0=ALU.mult, op1=ALU.add
+        )
+        lp_f = keep.tile([P, PACK], F32, name="lp_f")
+        nc.gpsimd.tensor_copy(out=lp_f[:], in_=lp_sb[:])
+
+        m_codes = keep.tile([P, C], U32, name="m_codes", align_bytes=64)
+        m_scales = keep.tile([P, C], U8, name="m_scales", align_bytes=64)
+        p_codes = keep.tile([P, C], U32, name="p_codes", align_bytes=64)
+        p_scales = keep.tile([P, C], U8, name="p_scales", align_bytes=64)
+        w_codes = keep.tile([P, O], U32, name="w_codes", align_bytes=64)
+        w_scales = keep.tile([P, O], U8, name="w_scales", align_bytes=64)
+        m_g = keep.tile([P, PACK * C], BF16, name="m_g", align_bytes=64)
+        p_g = keep.tile([P, PACK * C], BF16, name="p_g", align_bytes=64)
+        w_g = keep.tile([P, PACK * O], BF16, name="w_g", align_bytes=64)
+        p_w = keep.tile([P, PACK, C], BF16, name="p_w")
+        nps = keep.tile([P, PACK], F32, name="nps")
+        nc.vector.tensor_scalar(out=nps[:], in0=ps_sb[:], scalar1=-1.0, scalar2=None, op0=ALU.mult)
+        for t in range(PACK):
+            nc.vector.tensor_scalar(out=p_w[:, t, :], in0=pb_sb[:, t, :].bitcast(FP8), scalar1=nps[:, t : t + 1], scalar2=None, op0=ALU.mult)
+        nc.scalar.copy(
+            out=m_g[:].rearrange("p (s i t) -> p s i t", s=PACK, t=PACK),
+            in_=m_sb[:].rearrange("p t (i s) -> p s i t", s=PACK),
+        )
+        nc.vector.tensor_copy(
+            out=p_g[:].rearrange("p (s i t) -> p s i t", s=PACK, t=PACK),
+            in_=p_w[:].rearrange("p t (i s) -> p s i t", s=PACK),
+        )
+        nc.vector.quantize_mx(out=m_codes[:].bitcast(FP8X4), scales=m_scales[:], in_=m_g[:])
+        nc.vector.quantize_mx(out=p_codes[:].bitcast(FP8X4), scales=p_scales[:], in_=p_g[:])
+        nc.gpsimd.tensor_scalar(
+            out=w_g[:].rearrange("p (o t) -> p o t", t=PACK), in0=w_sb[:].rearrange("p t o -> p o t"), scalar1=1.0, scalar2=0.0, op0=ALU.mult, op1=ALU.add
+        )
+        nc.vector.quantize_mx(out=w_codes[:].bitcast(FP8X4), scales=w_scales[:], in_=w_g[:])
+
+        st = {}
+
+        def put(kind, i, t):
+            st[(kind, i)] = t
+            return t
+
+        def get(kind, i):
+            return st[(kind, i)]
+
+        def tx(i):
+            if i + 4 < PAIRS:
+                load(i + 4)
+            words = x_tiles[i][:].rearrange("p j d -> p (j d)").bitcast(F32)
+            xt = put("xt", i, psum.tile([P, TOK, 2], F32, name="xt"))
+            half = D // 2
+            for j in range(J):
+                for u in range(2):
+                    nc.tensor.transpose(xt[:, j * P : (j + 1) * P, u], words[:, j * half + u : (j + 1) * half : 2], ident[:])
+
+        def sq(i):
+            x2 = put("x2", i, work.tile([P, TOK * PACK], F32, name="x2"))
+            xb = get("xt", i)[:].rearrange("p r u -> p (r u)").bitcast(BF16)
+            nc.scalar.activation(out=x2[:], in_=xb, func=ACT.Square)
+
+        def h(i):
+            hk = put("hk", i, work.tile([P, 2, TOK * PACK], BF16, name="hk", align_bytes=64))
+            xb = get("xt", i)[:].rearrange("p r u -> p (r u)").bitcast(BF16)
+            nc.vector.tensor_tensor(out=hk[:, 0, :], in0=xb, in1=a_rep[:].rearrange("p r t -> p (r t)"), op=ALU.mult)
+
+        def k(i):
+            nc.vector.scalar_tensor_tensor(
+                out=get("hk", i)[:, 1, :], in0=get("x2", i)[:], scalar=-1.0, in1=a_rep[:].rearrange("p r t -> p (r t)"), op0=ALU.add, op1=ALU.mult
+            )
+
+        def qz(i):
+            codes = put("codes", i, work.tile([P, 2, TOK], U32, name="codes", align_bytes=64))
+            scales = put("scales", i, work.tile([P, 2, TOK], U8, name="scales", align_bytes=64))
+            nc.vector.quantize_mx(
+                out=codes[:].rearrange("p b r -> p (b r)").bitcast(FP8X4),
+                scales=scales[:].rearrange("p b r -> p (b r)"),
+                in_=get("hk", i)[:].rearrange("p b r -> p (b r)"),
+            )
+
+        def q_half(i, b):
+            qt = put(("qt", b), i, psum.tile([P, 2, TOK], F32, name="qt"))
+            codes, scales = get("codes", i), get("scales", i)
+            for s2 in range(2):
+                s = 2 * b + s2
+                cols = slice(s * P, (s + 1) * P)
+                for b2, (wc, ws) in enumerate(((m_codes, m_scales), (p_codes, p_scales))):
+                    nc.tensor.matmul_mx(
+                        out=qt[:, s2, :],
+                        lhsT=wc[:, cols].bitcast(FP8X4),
+                        lhsT_scale=ws[:, cols],
+                        rhs=codes[:, b2, :].bitcast(FP8X4),
+                        rhs_scale=scales[:, b2, :],
+                        start=(b2 == 0),
+                        stop=(b2 == 1),
+                    )
+
+        def lp_half(i, b):
+            if b == 0:
+                put("ql", i, work.tile([P, PACK, TOK], F32, name="ql"))
+            ql = get("ql", i)
+            qt = get(("qt", b), i)
+            for s2 in range(2):
+                s = 2 * b + s2
+                nc.scalar.activation(out=ql[:, s, :], in_=qt[:, s2, :], func=ACT.Identity, bias=lp_f[:, s : s + 1], scale=1.0)
+
+        def tq(i, j):
+            q = put(("q", j), i, psum.tile([P, C], F32, name="q"))
+            ql = get("ql", i)
+            for s in range(PACK):
+                nc.tensor.transpose(q[:, s * P : (s + 1) * P], ql[:, s, j * P : (j + 1) * P], ident[:])
+
+        def mx(i, j):
+            nm = put(("nm", j), i, work.tile([P, 1], F32, name="nm" + str(j)))
+            nc.vector.tensor_reduce(out=nm[:], in_=get(("q", j), i)[:], axis=AX.X, op=ALU.max, negate=True)
+
+        def ex(i, j):
+            e = put(("e", j), i, work.tile([P, C], F32, name="e" + str(j)))
+            ssum = put(("ssum", j), i, work.tile([P, 1], F32, name="ssum" + str(j)))
+            nc.scalar.activation(out=e[:], in_=get(("q", j), i)[:], func=ACT.Exp, bias=get(("nm", j), i)[:], scale=1.0, accum_out=ssum[:])
+
+        def rc(i, j):
+            rs = put(("rs", j), i, work.tile([P, 1], F32, name="rs" + str(j)))
+            nc.vector.reciprocal(out=rs[:], in_=get(("ssum", j), i)[:])
+
+        def us(i, j):
+            u = put(("u", j), i, work.tile([P, C], F32, name="u" + str(j)))
+            nc.gpsimd.tensor_scalar(
+                out=u[:], in0=get(("e", j), i)[:], scalar1=get(("rs", j), i)[:], scalar2=-1.0 / C, op0=ALU.mult, op1=ALU.add
+            )
+
+        def tu(i, j):
+            ut = put(("ut", j), i, psum.tile([P, PACK, P], F32, name="ut"))
+            u = get(("u", j), i)
+            for s in range(PACK):
+                nc.tensor.transpose(ut[:, s, :], u[:, s * P : (s + 1) * P], ident[:])
+
+        def rr(i, j):
+            if ("r", i) not in st:
+                put("r", i, work.tile([P, TOK, PACK], BF16, name="r", align_bytes=64))
+            nc.vector.tensor_tensor(
+                out=get("r", i)[:, j * P : (j + 1) * P, :], in0=get(("ut", j), i)[:].rearrange("p s n -> p n s"), in1=gc_rep[:], op=ALU.mult
+            )
+
+        def qr(i):
+            rcodes = put("rcodes", i, work.tile([P, TOK], U32, name="rcodes", align_bytes=64))
+            rscales = put("rscales", i, work.tile([P, TOK], U8, name="rscales", align_bytes=64))
+            nc.vector.quantize_mx(out=rcodes[:].bitcast(FP8X4), scales=rscales[:], in_=get("r", i)[:].rearrange("p n s -> p (n s)"))
+
+        def ou(i):
+            o_ps = put("o_ps", i, psum.tile([P, J, O], F32, name="ut"))
+            for j in range(J):
+                cols = slice(j * P, (j + 1) * P)
+                nc.tensor.matmul_mx(
+                    out=o_ps[:, j, :],
+                    lhsT=get("rcodes", i)[:, cols].bitcast(FP8X4),
+                    lhsT_scale=get("rscales", i)[:, cols],
+                    rhs=w_codes[:].bitcast(FP8X4),
+                    rhs_scale=w_scales[:],
+                    start=True,
+                    stop=True,
+                )
+
+        def co(i):
+            o_sb = work.tile([P, J, O], F32, name="o_sb")
+            nc.scalar.copy(out=o_sb[:], in_=get("o_ps", i)[:])
+            nc.sync.dma_start(out=out_v[i], in_=o_sb[:])
+
+        steps = {
+            "TX": tx, "SQ": sq, "H": h, "K": k, "QZ": qz,
+            "QA": lambda i: q_half(i, 0), "QB": lambda i: q_half(i, 1),
+            "LA": lambda i: lp_half(i, 0), "LB": lambda i: lp_half(i, 1),
+            "TQ0": lambda i: tq(i, 0), "TQ1": lambda i: tq(i, 1),
+            "M0": lambda i: mx(i, 0), "M1": lambda i: mx(i, 1),
+            "E0": lambda i: ex(i, 0), "E1": lambda i: ex(i, 1),
+            "C0": lambda i: rc(i, 0), "C1": lambda i: rc(i, 1),
+            "U0": lambda i: us(i, 0), "U1": lambda i: us(i, 1),
+            "TU0": lambda i: tu(i, 0), "TU1": lambda i: tu(i, 1),
+            "R0": lambda i: rr(i, 0), "R1": lambda i: rr(i, 1),
+            "QR": qr, "OU": ou, "CO": co,
+        }
+        with tc.manual_schedule():
+            for step in range(PAIRS + 3):
+                for name, off in ORDER:
+                    i = step - off
+                    if 0 <= i < PAIRS:
+                        steps[name](i)

@@ -23,9 +23,10 @@ TOK = J * P
 PAIRS = N // TOK
 
 ORDER = [
-    ("TX", 0), ("SQ", 0), ("TQ0", 2), ("R0", 3), ("TQ1", 2), ("TU1", 3), ("QZ", 1), ("M0", 2), ("E0", 2), ("M1", 2),
-    ("R1", 3), ("QA", 1), ("E1", 2), ("C0", 2), ("QR", 3), ("H", 0), ("LA", 1), ("C1", 2), ("QB", 1), ("K", 0),
-    ("LB", 1), ("U0", 2), ("OU", 3), ("U1", 2), ("TU0", 2), ("CO", 3),
+    ("U0", 4), ("I1", 5), ("LA", 2), ("TX", 0), ("QR", 5), ("E1", 3), ("TU1", 4), ("SQ", 0),
+    ("QZ", 1), ("TU0", 4), ("TQ0", 2), ("R1", 4), ("C", 3), ("TQ1", 2), ("M0", 2), ("R0", 4),
+    ("QB", 1), ("M1", 2), ("E0", 2), ("U1", 3), ("OU", 6), ("QA", 1), ("K", 0), ("H", 0),
+    ("LB", 1), ("CO", 6),
 ]
 
 
@@ -37,7 +38,7 @@ def tile_ellipticalnormalizedrbfnet_t_kernel(tc, x, a, m, p_bytes, p_scale, lp, 
     with ExitStack() as ctx:
         keep = ctx.enter_context(tc.tile_pool(name="keep", bufs=1))
         xin = ctx.enter_context(tc.tile_pool(name="xin", bufs=6))
-        work = ctx.enter_context(tc.tile_pool(name="work", bufs=3))
+        work = ctx.enter_context(tc.tile_pool(name="work", bufs=5))
         psum = ctx.enter_context(tc.psum_pool(name="psum", bufs=2))
 
         x_tiles = {}
@@ -81,6 +82,8 @@ def tile_ellipticalnormalizedrbfnet_t_kernel(tc, x, a, m, p_bytes, p_scale, lp, 
         nc.gpsimd.tensor_scalar(
             out=gc_rep[:], in0=gc_sb[:].unsqueeze(1).to_broadcast([P, P, PACK]), scalar1=float(C), scalar2=0.0, op0=ALU.mult, op1=ALU.add
         )
+        gc_f = keep.tile([P, PACK], F32, name="gc_f")
+        nc.gpsimd.tensor_scalar(out=gc_f[:], in0=gc_sb[:], scalar1=float(C), scalar2=0.0, op0=ALU.mult, op1=ALU.add)
         lp_f = keep.tile([P, PACK], F32, name="lp_f")
         nc.gpsimd.tensor_copy(out=lp_f[:], in_=lp_sb[:])
 
@@ -137,14 +140,19 @@ def tile_ellipticalnormalizedrbfnet_t_kernel(tc, x, a, m, p_bytes, p_scale, lp, 
             xb = get("xt", i)[:].rearrange("p r u -> p (r u)").bitcast(BF16)
             nc.scalar.activation(out=x2[:], in_=xb, func=ACT.Square)
 
+        def hk_tile(i):
+            if ("hk", i) not in st:
+                put("hk", i, work.tile([P, 2, TOK * PACK], BF16, name="hk", align_bytes=64))
+            return get("hk", i)
+
         def h(i):
-            hk = put("hk", i, work.tile([P, 2, TOK * PACK], BF16, name="hk", align_bytes=64))
+            hk = hk_tile(i)
             xb = get("xt", i)[:].rearrange("p r u -> p (r u)").bitcast(BF16)
             nc.vector.tensor_tensor(out=hk[:, 0, :], in0=xb, in1=a_rep[:].rearrange("p r t -> p (r t)"), op=ALU.mult)
 
         def k(i):
             nc.vector.scalar_tensor_tensor(
-                out=get("hk", i)[:, 1, :], in0=get("x2", i)[:], scalar=-1.0, in1=a_rep[:].rearrange("p r t -> p (r t)"), op0=ALU.add, op1=ALU.mult
+                out=hk_tile(i)[:, 1, :], in0=get("x2", i)[:], scalar=-1.0, in1=a_rep[:].rearrange("p r t -> p (r t)"), op0=ALU.add, op1=ALU.mult
             )
 
         def qz(i):
@@ -174,7 +182,7 @@ def tile_ellipticalnormalizedrbfnet_t_kernel(tc, x, a, m, p_bytes, p_scale, lp, 
                     )
 
         def lp_half(i, b):
-            if b == 0:
+            if ("ql", i) not in st:
                 put("ql", i, work.tile([P, PACK, TOK], F32, name="ql"))
             ql = get("ql", i)
             qt = get(("qt", b), i)
@@ -194,17 +202,19 @@ def tile_ellipticalnormalizedrbfnet_t_kernel(tc, x, a, m, p_bytes, p_scale, lp, 
 
         def ex(i, j):
             e = put(("e", j), i, work.tile([P, C], F32, name="e" + str(j)))
-            ssum = put(("ssum", j), i, work.tile([P, 1], F32, name="ssum" + str(j)))
-            nc.scalar.activation(out=e[:], in_=get(("q", j), i)[:], func=ACT.Exp, bias=get(("nm", j), i)[:], scale=1.0, accum_out=ssum[:])
+            if ("ssum", i) not in st:
+                put("ssum", i, work.tile([P, J], F32, name="ssum"))
+            ssum = get("ssum", i)
+            nc.scalar.activation(out=e[:], in_=get(("q", j), i)[:], func=ACT.Exp, bias=get(("nm", j), i)[:], scale=1.0, accum_out=ssum[:, j : j + 1])
 
-        def rc(i, j):
-            rs = put(("rs", j), i, work.tile([P, 1], F32, name="rs" + str(j)))
-            nc.vector.reciprocal(out=rs[:], in_=get(("ssum", j), i)[:])
+        def rc(i):
+            rs = put("rs", i, work.tile([P, J], F32, name="rs"))
+            nc.vector.reciprocal(out=rs[:], in_=get("ssum", i)[:])
 
         def us(i, j):
             u = put(("u", j), i, work.tile([P, C], F32, name="u" + str(j)))
             nc.gpsimd.tensor_scalar(
-                out=u[:], in0=get(("e", j), i)[:], scalar1=get(("rs", j), i)[:], scalar2=-1.0 / C, op0=ALU.mult, op1=ALU.add
+                out=u[:], in0=get(("e", j), i)[:], scalar1=get("rs", i)[:, j : j + 1], scalar2=-1.0 / C, op0=ALU.mult, op1=ALU.add
             )
 
         def tu(i, j):
@@ -219,6 +229,19 @@ def tile_ellipticalnormalizedrbfnet_t_kernel(tc, x, a, m, p_bytes, p_scale, lp, 
             nc.vector.tensor_tensor(
                 out=get("r", i)[:, j * P : (j + 1) * P, :], in0=get(("ut", j), i)[:].rearrange("p s n -> p n s"), in1=gc_rep[:], op=ALU.mult
             )
+
+        def ra(i, j):
+            rp = put("rp", i, work.tile([P, PACK, P], BF16, name="rp"))
+            ut = get(("ut", j), i)
+            for s in range(PACK):
+                nc.scalar.activation(out=rp[:, s, :], in_=ut[:, s, :], func=ACT.Copy, scale=gc_f[:, s : s + 1])
+
+        def il(i, j):
+            if ("r", i) not in st:
+                put("r", i, work.tile([P, TOK, PACK], BF16, name="r", align_bytes=64))
+            o_v = get("r", i)[:, j * P : (j + 1) * P, :]
+            i_v = get("rp", i)[:].rearrange("p s n -> p n s")
+            nc.gpsimd.tensor_scalar(out=o_v, in0=i_v, scalar1=1.0, scalar2=0.0, op0=ALU.mult, op1=ALU.add)
 
         def qr(i):
             rcodes = put("rcodes", i, work.tile([P, TOK], U32, name="rcodes", align_bytes=64))
@@ -251,14 +274,14 @@ def tile_ellipticalnormalizedrbfnet_t_kernel(tc, x, a, m, p_bytes, p_scale, lp, 
             "TQ0": lambda i: tq(i, 0), "TQ1": lambda i: tq(i, 1),
             "M0": lambda i: mx(i, 0), "M1": lambda i: mx(i, 1),
             "E0": lambda i: ex(i, 0), "E1": lambda i: ex(i, 1),
-            "C0": lambda i: rc(i, 0), "C1": lambda i: rc(i, 1),
+            "C": rc,
             "U0": lambda i: us(i, 0), "U1": lambda i: us(i, 1),
             "TU0": lambda i: tu(i, 0), "TU1": lambda i: tu(i, 1),
-            "R0": lambda i: rr(i, 0), "R1": lambda i: rr(i, 1),
+            "R0": lambda i: rr(i, 0), "R1": lambda i: ra(i, 1), "I1": lambda i: il(i, 1),
             "QR": qr, "OU": ou, "CO": co,
         }
         with tc.manual_schedule():
-            for step in range(PAIRS + 3):
+            for step in range(PAIRS + 6):
                 for name, off in ORDER:
                     i = step - off
                     if 0 <= i < PAIRS:

@@ -23,10 +23,10 @@ TOK = J * P
 PAIRS = N // TOK
 
 ORDER = [
-    ("U0", 4), ("I1", 5), ("LA", 2), ("TX", 0), ("QR", 5), ("E1", 3), ("TU1", 4), ("SQ", 0),
-    ("QZ", 1), ("TU0", 4), ("TQ0", 2), ("R1", 4), ("C", 3), ("TQ1", 2), ("M0", 2), ("R0", 4),
-    ("QB", 1), ("M1", 2), ("E0", 2), ("U1", 3), ("OU", 6), ("QA", 1), ("K", 0), ("H", 0),
-    ("LB", 1), ("CO", 6),
+    ("QZ", 2), ("TX", 0), ("TU1", 5), ("TQ0", 3), ("K", 1), ("I1", 6), ("SQ", 0), ("C", 4),
+    ("TQ1", 3), ("M0", 3), ("TU0", 5), ("R1", 5), ("QR", 6), ("E0", 3), ("QA", 2), ("LA", 2),
+    ("QB", 2), ("M1", 3), ("OU", 6), ("U1", 4), ("LB", 2), ("E1", 3), ("CO", 6), ("H", 0),
+    ("U0", 4), ("R0", 5),
 ]
 
 
@@ -277,7 +277,7 @@ def tile_ellipticalnormalizedrbfnet_t_kernel(tc, x, a, m, p_bytes, p_scale, lp, 
             "C": rc,
             "U0": lambda i: us(i, 0), "U1": lambda i: us(i, 1),
             "TU0": lambda i: tu(i, 0), "TU1": lambda i: tu(i, 1),
-            "R0": lambda i: rr(i, 0), "R1": lambda i: ra(i, 1), "I1": lambda i: il(i, 1),
+            "R0": lambda i: rr(i, 0), "R1": lambda i: rr(i, 1) if i % 4 == 3 else ra(i, 1), "I1": lambda i: None if i % 4 == 3 else il(i, 1),
             "QR": qr, "OU": ou, "CO": co,
         }
         with tc.manual_schedule():

from contextlib import ExitStack

import concourse.mybir as mybir
from concourse.masks import make_identity

N, D, C, O = 8192, 512, 512, 256
FLOPS = 2 * N * D * C * 2 + 2 * N * C * O

F32 = mybir.dt.float32
BF16 = mybir.dt.bfloat16
U32 = mybir.dt.uint32
U8 = mybir.dt.uint8
FP8 = mybir.dt.float8_e4m3fn
FP8X4 = mybir.dt.float8_e4m3fn_x4
ACT = mybir.ActivationFunctionType
ALU = mybir.AluOpType
AX = mybir.AxisListType

P = 128
PACK = 4
J = 2
TOK = J * P
PAIRS = N // TOK

ORDER = [
    ("QZ", 2), ("TX", 0), ("TU1", 5), ("TQ0", 3), ("K", 1), ("I1", 6), ("SQ", 0), ("C", 4),
    ("TQ1", 3), ("M0", 3), ("TU0", 5), ("R1", 5), ("QR", 6), ("E0", 3), ("QA", 2), ("LA", 2),
    ("QB", 2), ("M1", 3), ("OU", 6), ("U1", 4), ("LB", 2), ("E1", 3), ("CO", 6), ("H", 0),
    ("U0", 4), ("R0", 5),
]


def tile_ellipticalnormalizedrbfnet_t_kernel(tc, x, a, m, p_bytes, p_scale, lp, gc, w, out):
    nc = tc.nc
    x_v = x.rearrange("(g p j) d -> g p j d", p=P, j=J)
    out_v = out.rearrange("(g p j) o -> g p j o", p=P, j=J)

    with ExitStack() as ctx:
        keep = ctx.enter_context(tc.tile_pool(name="keep", bufs=1))
        xin = ctx.enter_context(tc.tile_pool(name="xin", bufs=6))
        work = ctx.enter_context(tc.tile_pool(name="work", bufs=5))
        psum = ctx.enter_context(tc.psum_pool(name="psum", bufs=2))

        x_tiles = {}

        def load(i):
            x_sb = xin.tile([P, J, D], BF16, name="x_sb")
            nc.sync.dma_start(out=x_sb[:], in_=x_v[i])
            x_tiles[i] = x_sb

        ident = keep.tile([P, P], F32, name="ident")
        make_identity(nc, ident[:])
        warm = keep.tile([P, 1], F32, name="warm")
        nc.gpsimd.memset(warm[:], 0.0)
        warm2 = keep.tile([P, 1], F32, name="warm2")
        nc.scalar.activation(out=warm2[:], in_=warm[:], func=ACT.Exp, bias=0.0, scale=1.0)

        load(0)
        a_sb = keep.tile([P, PACK], BF16, name="a_sb")
        nc.sync.dma_start(out=a_sb[:], in_=a.rearrange("(p t) -> p t", t=PACK))
        ps_sb = keep.tile([P, PACK], F32, name="ps_sb")
        nc.sync.dma_start(out=ps_sb[:], in_=p_scale.rearrange("(p t) o -> p (t o)", t=PACK))
        pb_sb = keep.tile([P, PACK, C], U8, name="pb_sb")
        nc.sync.dma_start(out=pb_sb[:], in_=p_bytes.rearrange("(p t) c -> p t c", t=PACK))
        m_sb = keep.tile([P, PACK, C], BF16, name="m_sb")
        nc.sync.dma_start(out=m_sb[:], in_=m.rearrange("(p t) c -> p t c", t=PACK))
        lp_sb = keep.tile([P, PACK], BF16, name="lp_sb")
        nc.sync.dma_start(out=lp_sb[:], in_=lp.rearrange("(p t) -> p t", t=PACK))
        gc_sb = keep.tile([P, PACK], BF16, name="gc_sb")
        nc.sync.dma_start(out=gc_sb[:], in_=gc.rearrange("(p t) -> p t", t=PACK))
        load(1)
        w_sb = keep.tile([P, PACK, O], BF16, name="w_sb")
        nc.sync.dma_start(out=w_sb[:], in_=w.rearrange("(p t) o -> p t o", t=PACK))
        load(2)
        load(3)

        a_rep = keep.tile([P, TOK, PACK], BF16, name="a_rep", align_bytes=64)
        nc.gpsimd.tensor_scalar(
            out=a_rep[:], in0=a_sb[:].unsqueeze(1).to_broadcast([P, TOK, PACK]), scalar1=1.0, scalar2=0.0, op0=ALU.mult, op1=ALU.add
        )
        gc_rep = keep.tile([P, P, PACK], F32, name="gc_rep", align_bytes=64)
        nc.gpsimd.tensor_scalar(
            out=gc_rep[:], in0=gc_sb[:].unsqueeze(1).to_broadcast([P, P, PACK]), scalar1=float(C), scalar2=0.0, op0=ALU.mult, op1=ALU.add
        )
        gc_f = keep.tile([P, PACK], F32, name="gc_f")
        nc.gpsimd.tensor_scalar(out=gc_f[:], in0=gc_sb[:], scalar1=float(C), scalar2=0.0, op0=ALU.mult, op1=ALU.add)
        lp_f = keep.tile([P, PACK], F32, name="lp_f")
        nc.gpsimd.tensor_copy(out=lp_f[:], in_=lp_sb[:])

        m_codes = keep.tile([P, C], U32, name="m_codes", align_bytes=64)
        m_scales = keep.tile([P, C], U8, name="m_scales", align_bytes=64)
        p_codes = keep.tile([P, C], U32, name="p_codes", align_bytes=64)
        p_scales = keep.tile([P, C], U8, name="p_scales", align_bytes=64)
        w_codes = keep.tile([P, O], U32, name="w_codes", align_bytes=64)
        w_scales = keep.tile([P, O], U8, name="w_scales", align_bytes=64)
        m_g = keep.tile([P, PACK * C], BF16, name="m_g", align_bytes=64)
        p_g = keep.tile([P, PACK * C], BF16, name="p_g", align_bytes=64)
        w_g = keep.tile([P, PACK * O], BF16, name="w_g", align_bytes=64)
        p_w = keep.tile([P, PACK, C], BF16, name="p_w")
        nps = keep.tile([P, PACK], F32, name="nps")
        nc.vector.tensor_scalar(out=nps[:], in0=ps_sb[:], scalar1=-1.0, scalar2=None, op0=ALU.mult)
        for t in range(PACK):
            nc.vector.tensor_scalar(out=p_w[:, t, :], in0=pb_sb[:, t, :].bitcast(FP8), scalar1=nps[:, t : t + 1], scalar2=None, op0=ALU.mult)
        nc.scalar.copy(
            out=m_g[:].rearrange("p (s i t) -> p s i t", s=PACK, t=PACK),
            in_=m_sb[:].rearrange("p t (i s) -> p s i t", s=PACK),
        )
        nc.vector.tensor_copy(
            out=p_g[:].rearrange("p (s i t) -> p s i t", s=PACK, t=PACK),
            in_=p_w[:].rearrange("p t (i s) -> p s i t", s=PACK),
        )
        nc.vector.quantize_mx(out=m_codes[:].bitcast(FP8X4), scales=m_scales[:], in_=m_g[:])
        nc.vector.quantize_mx(out=p_codes[:].bitcast(FP8X4), scales=p_scales[:], in_=p_g[:])
        nc.gpsimd.tensor_scalar(
            out=w_g[:].rearrange("p (o t) -> p o t", t=PACK), in0=w_sb[:].rearrange("p t o -> p o t"), scalar1=1.0, scalar2=0.0, op0=ALU.mult, op1=ALU.add
        )
        nc.vector.quantize_mx(out=w_codes[:].bitcast(FP8X4), scales=w_scales[:], in_=w_g[:])

        st = {}

        def put(kind, i, t):
            st[(kind, i)] = t
            return t

        def get(kind, i):
            return st[(kind, i)]

        def tx(i):
            if i + 4 < PAIRS:
                load(i + 4)
            words = x_tiles[i][:].rearrange("p j d -> p (j d)").bitcast(F32)
            xt = put("xt", i, psum.tile([P, TOK, 2], F32, name="xt"))
            half = D // 2
            for j in range(J):
                for u in range(2):
                    nc.tensor.transpose(xt[:, j * P : (j + 1) * P, u], words[:, j * half + u : (j + 1) * half : 2], ident[:])

        def sq(i):
            x2 = put("x2", i, work.tile([P, TOK * PACK], F32, name="x2"))
            xb = get("xt", i)[:].rearrange("p r u -> p (r u)").bitcast(BF16)
            nc.scalar.activation(out=x2[:], in_=xb, func=ACT.Square)

        def hk_tile(i):
            if ("hk", i) not in st:
                put("hk", i, work.tile([P, 2, TOK * PACK], BF16, name="hk", align_bytes=64))
            return get("hk", i)

        def h(i):
            hk = hk_tile(i)
            xb = get("xt", i)[:].rearrange("p r u -> p (r u)").bitcast(BF16)
            nc.vector.tensor_tensor(out=hk[:, 0, :], in0=xb, in1=a_rep[:].rearrange("p r t -> p (r t)"), op=ALU.mult)

        def k(i):
            nc.vector.scalar_tensor_tensor(
                out=hk_tile(i)[:, 1, :], in0=get("x2", i)[:], scalar=-1.0, in1=a_rep[:].rearrange("p r t -> p (r t)"), op0=ALU.add, op1=ALU.mult
            )

        def qz(i):
            codes = put("codes", i, work.tile([P, 2, TOK], U32, name="codes", align_bytes=64))
            scales = put("scales", i, work.tile([P, 2, TOK], U8, name="scales", align_bytes=64))
            nc.vector.quantize_mx(
                out=codes[:].rearrange("p b r -> p (b r)").bitcast(FP8X4),
                scales=scales[:].rearrange("p b r -> p (b r)"),
                in_=get("hk", i)[:].rearrange("p b r -> p (b r)"),
            )

        def q_half(i, b):
            qt = put(("qt", b), i, psum.tile([P, 2, TOK], F32, name="qt"))
            codes, scales = get("codes", i), get("scales", i)
            for s2 in range(2):
                s = 2 * b + s2
                cols = slice(s * P, (s + 1) * P)
                for b2, (wc, ws) in enumerate(((m_codes, m_scales), (p_codes, p_scales))):
                    nc.tensor.matmul_mx(
                        out=qt[:, s2, :],
                        lhsT=wc[:, cols].bitcast(FP8X4),
                        lhsT_scale=ws[:, cols],
                        rhs=codes[:, b2, :].bitcast(FP8X4),
                        rhs_scale=scales[:, b2, :],
                        start=(b2 == 0),
                        stop=(b2 == 1),
                    )

        def lp_half(i, b):
            if ("ql", i) not in st:
                put("ql", i, work.tile([P, PACK, TOK], F32, name="ql"))
            ql = get("ql", i)
            qt = get(("qt", b), i)
            for s2 in range(2):
                s = 2 * b + s2
                nc.scalar.activation(out=ql[:, s, :], in_=qt[:, s2, :], func=ACT.Identity, bias=lp_f[:, s : s + 1], scale=1.0)

        def tq(i, j):
            q = put(("q", j), i, psum.tile([P, C], F32, name="q"))
            ql = get("ql", i)
            for s in range(PACK):
                nc.tensor.transpose(q[:, s * P : (s + 1) * P], ql[:, s, j * P : (j + 1) * P], ident[:])

        def mx(i, j):
            nm = put(("nm", j), i, work.tile([P, 1], F32, name="nm" + str(j)))
            nc.vector.tensor_reduce(out=nm[:], in_=get(("q", j), i)[:], axis=AX.X, op=ALU.max, negate=True)

        def ex(i, j):
            e = put(("e", j), i, work.tile([P, C], F32, name="e" + str(j)))
            if ("ssum", i) not in st:
                put("ssum", i, work.tile([P, J], F32, name="ssum"))
            ssum = get("ssum", i)
            nc.scalar.activation(out=e[:], in_=get(("q", j), i)[:], func=ACT.Exp, bias=get(("nm", j), i)[:], scale=1.0, accum_out=ssum[:, j : j + 1])

        def rc(i):
            rs = put("rs", i, work.tile([P, J], F32, name="rs"))
            nc.vector.reciprocal(out=rs[:], in_=get("ssum", i)[:])

        def us(i, j):
            u = put(("u", j), i, work.tile([P, C], F32, name="u" + str(j)))
            nc.gpsimd.tensor_scalar(
                out=u[:], in0=get(("e", j), i)[:], scalar1=get("rs", i)[:, j : j + 1], scalar2=-1.0 / C, op0=ALU.mult, op1=ALU.add
            )

        def tu(i, j):
            ut = put(("ut", j), i, psum.tile([P, PACK, P], F32, name="ut"))
            u = get(("u", j), i)
            for s in range(PACK):
                nc.tensor.transpose(ut[:, s, :], u[:, s * P : (s + 1) * P], ident[:])

        def rr(i, j):
            if ("r", i) not in st:
                put("r", i, work.tile([P, TOK, PACK], BF16, name="r", align_bytes=64))
            nc.vector.tensor_tensor(
                out=get("r", i)[:, j * P : (j + 1) * P, :], in0=get(("ut", j), i)[:].rearrange("p s n -> p n s"), in1=gc_rep[:], op=ALU.mult
            )

        def ra(i, j):
            rp = put("rp", i, work.tile([P, PACK, P], BF16, name="rp"))
            ut = get(("ut", j), i)
            for s in range(PACK):
                nc.scalar.activation(out=rp[:, s, :], in_=ut[:, s, :], func=ACT.Copy, scale=gc_f[:, s : s + 1])

        def il(i, j):
            if ("r", i) not in st:
                put("r", i, work.tile([P, TOK, PACK], BF16, name="r", align_bytes=64))
            o_v = get("r", i)[:, j * P : (j + 1) * P, :]
            i_v = get("rp", i)[:].rearrange("p s n -> p n s")
            nc.gpsimd.tensor_scalar(out=o_v, in0=i_v, scalar1=1.0, scalar2=0.0, op0=ALU.mult, op1=ALU.add)

        def qr(i):
            rcodes = put("rcodes", i, work.tile([P, TOK], U32, name="rcodes", align_bytes=64))
            rscales = put("rscales", i, work.tile([P, TOK], U8, name="rscales", align_bytes=64))
            nc.vector.quantize_mx(out=rcodes[:].bitcast(FP8X4), scales=rscales[:], in_=get("r", i)[:].rearrange("p n s -> p (n s)"))

        def ou(i):
            o_ps = put("o_ps", i, psum.tile([P, J, O], F32, name="ut"))
            for j in range(J):
                cols = slice(j * P, (j + 1) * P)
                nc.tensor.matmul_mx(
                    out=o_ps[:, j, :],
                    lhsT=get("rcodes", i)[:, cols].bitcast(FP8X4),
                    lhsT_scale=get("rscales", i)[:, cols],
                    rhs=w_codes[:].bitcast(FP8X4),
                    rhs_scale=w_scales[:],
                    start=True,
                    stop=True,
                )

        def co(i):
            o_sb = work.tile([P, J, O], F32, name="o_sb")
            nc.scalar.copy(out=o_sb[:], in_=get("o_ps", i)[:])
            nc.sync.dma_start(out=out_v[i], in_=o_sb[:])

        steps = {
            "TX": tx, "SQ": sq, "H": h, "K": k, "QZ": qz,
            "QA": lambda i: q_half(i, 0), "QB": lambda i: q_half(i, 1),
            "LA": lambda i: lp_half(i, 0), "LB": lambda i: lp_half(i, 1),
            "TQ0": lambda i: tq(i, 0), "TQ1": lambda i: tq(i, 1),
            "M0": lambda i: mx(i, 0), "M1": lambda i: mx(i, 1),
            "E0": lambda i: ex(i, 0), "E1": lambda i: ex(i, 1),
            "C": rc,
            "U0": lambda i: us(i, 0), "U1": lambda i: us(i, 1),
            "TU0": lambda i: tu(i, 0), "TU1": lambda i: tu(i, 1),
            "R0": lambda i: rr(i, 0), "R1": lambda i: rr(i, 1) if i % 4 == 3 else ra(i, 1), "I1": lambda i: None if i % 4 == 3 else il(i, 1),
            "QR": qr, "OU": ou, "CO": co,
        }
        with tc.manual_schedule():
            for step in range(PAIRS + 6):
                for name, off in ORDER:
                    i = step - off
                    if 0 <= i < PAIRS:
                        steps[name](i)
